import numpy as np
CORES = [4,132,260,388,12,140,268,396,20,148,276,404,28,156,284,412]
N = 16
def setup_inputs(rng):
    return {"x": rng.standard_normal((N, 128, 4), dtype=np.float32)}
def reference(x):
    s = x.sum(axis=0, dtype=np.float64).astype(x.dtype)
    return {"y": np.broadcast_to(s, (N,) + s.shape)}

@@ -1,0 +1,56 @@
+from concourse.bass import DstId, RemoteDMATransfer
+
+W = 4
+SCRATCH = {
+    "xs": ("dram", [128, W], "float32"),
+    "raw": ("dram", [4, 128, W], "float32"),
+    "part": ("dram", [3, 128, W], "float32"),
+    "res": ("dram", [128, W], "float32"),
+}
+SEMAPHORES = ["loaded", "sent", "rawin", "partin", "fin", "stored"]
+
+RANK_CORE, HELP_CORE = 4, 6
+
+
+def _world(h, c, k):
+    return h * 128 + c * 8 + k
+
+
+def _bits(m):
+    return bin(m).count("1")
+
+
+def rank_program(g, core, T, topo):
+    h, c, k = topo.host(core), topo.chip(core), core % 8
+    if c > 3 or k not in (RANK_CORE, HELP_CORE):
+        return
+
+    def dst(d):
+        rid, pid = topo.addr(d, core)
+        return DstId(rid=rid, pnc=pid)
+
+    if k == RANK_CORE:
+        g.sync.dma_start(T.xs[:], T.x[:]).then_inc(T.sem.loaded, 16)
+        slot = (h & 1) * 2 + (c >> 1)
+        plan = [((h, c), 0xFF00), ((h, c ^ 2), 0x0003), ((h ^ 1, c), 0x000C), ((h ^ 1, c ^ 2), 0x00F0)]
+        trs = [RemoteDMATransfer(dst_ids=[dst(_world(hh, cc, HELP_CORE))], dma_engine_mask=m, remote_sem=T.sem.rawin,
+                                 src=T.xs[:], dst=T.raw[slot]) for (hh, cc), m in plan]
+        g.wait_ge(T.sem.loaded, 16)
+        g.remote_dma_fused(trs, local_sem=T.sem.sent)
+        g.sync.wait_ge(T.sem.fin, 16)
+        g.sync.dma_start(T.y[:], T.res[:]).then_inc(T.sem.stored, 16)
+        g.sync.wait_ge(T.sem.stored, 16)
+        g.wait_ge(T.sem.sent, sum(_bits(m) for _, m in plan))
+        return
+
+    raws = [T.raw[i] for i in range(4)]
+    plan = [((h, c ^ 1), 0x0003, 0), ((3 - h, c), 0x000C, 1), ((3 - h, c ^ 1), 0x00F0, 2)]
+    trs = [RemoteDMATransfer(dst_ids=[dst(_world(hh, cc, HELP_CORE))], dma_engine_mask=m, remote_sem=T.sem.partin,
+                             srcs=raws, dsts=[T.part[s]], alu_op=1) for (hh, cc), m, s in plan]
+    g.wait_ge(T.sem.rawin, 16)
+    g.remote_dma_fused(trs, local_sem=T.sem.sent)
+    last = RemoteDMATransfer(dst_ids=[dst(_world(h, c, RANK_CORE))], dma_engine_mask=0xFFFF, remote_sem=T.sem.fin,
+                             srcs=raws + [T.part[s] for s in range(3)], dsts=[T.res[:]], alu_op=1)
+    g.wait_ge(T.sem.partin, 8)
+    g.remote_dma_fused([last], local_sem=T.sem.sent)
+    g.wait_ge(T.sem.sent, 8 + 16)

@@ -16,10 +16,6 @@ def _world(h, c, k):
     return h * 128 + c * 8 + k
 
 
-def _bits(m):
-    return bin(m).count("1")
-
-
 def rank_program(g, core, T, topo):
     h, c, k = topo.host(core), topo.chip(core), core % 8
     if c > 3 or k not in (RANK_CORE, HELP_CORE):
@@ -32,25 +28,25 @@ def rank_program(g, core, T, topo):
     if k == RANK_CORE:
         g.sync.dma_start(T.xs[:], T.x[:]).then_inc(T.sem.loaded, 16)
         slot = (h & 1) * 2 + (c >> 1)
-        plan = [((h, c), 0xFF00), ((h, c ^ 2), 0x0003), ((h ^ 1, c), 0x000C), ((h ^ 1, c ^ 2), 0x00F0)]
-        trs = [RemoteDMATransfer(dst_ids=[dst(_world(hh, cc, HELP_CORE))], dma_engine_mask=m, remote_sem=T.sem.rawin,
-                                 src=T.xs[:], dst=T.raw[slot]) for (hh, cc), m in plan]
+        plan = [(h, c), (h, c ^ 2), (h ^ 1, c), (h ^ 1, c ^ 2)]
+        tr = RemoteDMATransfer(dst_ids=[dst(_world(hh, cc, HELP_CORE)) for hh, cc in plan], dma_engine_mask=0xFF,
+                               remote_sem=T.sem.rawin, srcs=[T.xs[:]], dsts=[T.raw[slot]] * 4)
         g.wait_ge(T.sem.loaded, 16)
-        g.remote_dma_fused(trs, local_sem=T.sem.sent)
+        g.remote_dma_fused([tr], local_sem=T.sem.sent)
         g.sync.wait_ge(T.sem.fin, 16)
         g.sync.dma_start(T.y[:], T.res[:]).then_inc(T.sem.stored, 16)
         g.sync.wait_ge(T.sem.stored, 16)
-        g.wait_ge(T.sem.sent, sum(_bits(m) for _, m in plan))
+        g.wait_ge(T.sem.sent, 8)
         return
 
     raws = [T.raw[i] for i in range(4)]
-    plan = [((h, c ^ 1), 0x0003, 0), ((3 - h, c), 0x000C, 1), ((3 - h, c ^ 1), 0x00F0, 2)]
-    trs = [RemoteDMATransfer(dst_ids=[dst(_world(hh, cc, HELP_CORE))], dma_engine_mask=m, remote_sem=T.sem.partin,
-                             srcs=raws, dsts=[T.part[s]], alu_op=1) for (hh, cc), m, s in plan]
-    g.wait_ge(T.sem.rawin, 16)
-    g.remote_dma_fused(trs, local_sem=T.sem.sent)
+    plan = [((h, c ^ 1), 0), ((3 - h, c), 1), ((3 - h, c ^ 1), 2)]
+    tr = RemoteDMATransfer(dst_ids=[dst(_world(hh, cc, HELP_CORE)) for (hh, cc), s in plan], dma_engine_mask=0xFF,
+                           remote_sem=T.sem.partin, srcs=raws, dsts=[T.part[s] for _, s in plan], alu_op=1)
+    g.wait_ge(T.sem.rawin, 4 * 8)
+    g.remote_dma_fused([tr], local_sem=T.sem.sent)
     last = RemoteDMATransfer(dst_ids=[dst(_world(h, c, RANK_CORE))], dma_engine_mask=0xFFFF, remote_sem=T.sem.fin,
                              srcs=raws + [T.part[s] for s in range(3)], dsts=[T.res[:]], alu_op=1)
-    g.wait_ge(T.sem.partin, 8)
+    g.wait_ge(T.sem.partin, 3 * 8)
     g.remote_dma_fused([last], local_sem=T.sem.sent)
     g.wait_ge(T.sem.sent, 8 + 16)

@@ -28,7 +28,7 @@ def rank_program(g, core, T, topo):
     if k == RANK_CORE:
         g.sync.dma_start(T.xs[:], T.x[:]).then_inc(T.sem.loaded, 16)
         slot = (h & 1) * 2 + (c >> 1)
-        plan = [(h, c), (h, c ^ 2), (h ^ 1, c), (h ^ 1, c ^ 2)]
+        plan = [(h ^ 1, c ^ 2), (h ^ 1, c), (h, c ^ 2), (h, c)]
         tr = RemoteDMATransfer(dst_ids=[dst(_world(hh, cc, HELP_CORE)) for hh, cc in plan], dma_engine_mask=0xFF,
                                remote_sem=T.sem.rawin, srcs=[T.xs[:]], dsts=[T.raw[slot]] * 4)
         g.wait_ge(T.sem.loaded, 16)
@@ -40,7 +40,7 @@ def rank_program(g, core, T, topo):
         return
 
     raws = [T.raw[i] for i in range(4)]
-    plan = [((h, c ^ 1), 0), ((3 - h, c), 1), ((3 - h, c ^ 1), 2)]
+    plan = [((3 - h, c ^ 1), 2), ((3 - h, c), 1), ((h, c ^ 1), 0)]
     tr = RemoteDMATransfer(dst_ids=[dst(_world(hh, cc, HELP_CORE)) for (hh, cc), s in plan], dma_engine_mask=0xFF,
                            remote_sem=T.sem.partin, srcs=raws, dsts=[T.part[s] for _, s in plan], alu_op=1)
     g.wait_ge(T.sem.rawin, 4 * 8)

from concourse.bass import DstId, RemoteDMATransfer

W = 4
SCRATCH = {
    "xs": ("dram", [128, W], "float32"),
    "raw": ("dram", [4, 128, W], "float32"),
    "part": ("dram", [3, 128, W], "float32"),
    "res": ("dram", [128, W], "float32"),
}
SEMAPHORES = ["loaded", "sent", "rawin", "partin", "fin", "stored"]

RANK_CORE, HELP_CORE = 4, 6


def _world(h, c, k):
    return h * 128 + c * 8 + k


def rank_program(g, core, T, topo):
    h, c, k = topo.host(core), topo.chip(core), core % 8
    if c > 3 or k not in (RANK_CORE, HELP_CORE):
        return

    def dst(d):
        rid, pid = topo.addr(d, core)
        return DstId(rid=rid, pnc=pid)

    if k == RANK_CORE:
        g.sync.dma_start(T.xs[:], T.x[:]).then_inc(T.sem.loaded, 16)
        slot = (h & 1) * 2 + (c >> 1)
        plan = [(h ^ 1, c ^ 2), (h ^ 1, c), (h, c ^ 2), (h, c)]
        tr = RemoteDMATransfer(dst_ids=[dst(_world(hh, cc, HELP_CORE)) for hh, cc in plan], dma_engine_mask=0xFF,
                               remote_sem=T.sem.rawin, srcs=[T.xs[:]], dsts=[T.raw[slot]] * 4)
        g.wait_ge(T.sem.loaded, 16)
        g.remote_dma_fused([tr], local_sem=T.sem.sent)
        g.sync.wait_ge(T.sem.fin, 16)
        g.sync.dma_start(T.y[:], T.res[:]).then_inc(T.sem.stored, 16)
        g.sync.wait_ge(T.sem.stored, 16)
        g.wait_ge(T.sem.sent, 8)
        return

    raws = [T.raw[i] for i in range(4)]
    plan = [((3 - h, c ^ 1), 2), ((3 - h, c), 1), ((h, c ^ 1), 0)]
    tr = RemoteDMATransfer(dst_ids=[dst(_world(hh, cc, HELP_CORE)) for (hh, cc), s in plan], dma_engine_mask=0xFF,
                           remote_sem=T.sem.partin, srcs=raws, dsts=[T.part[s] for _, s in plan], alu_op=1)
    g.wait_ge(T.sem.rawin, 4 * 8)
    g.remote_dma_fused([tr], local_sem=T.sem.sent)
    last = RemoteDMATransfer(dst_ids=[dst(_world(h, c, RANK_CORE))], dma_engine_mask=0xFFFF, remote_sem=T.sem.fin,
                             srcs=raws + [T.part[s] for s in range(3)], dsts=[T.res[:]], alu_op=1)
    g.wait_ge(T.sem.partin, 3 * 8)
    g.remote_dma_fused([last], local_sem=T.sem.sent)
    g.wait_ge(T.sem.sent, 8 + 16)
